import numpy as np
import ml_dtypes


def mxq(x, axis, fmt="e4m3"):
    dtype, down = {"e4m3": (ml_dtypes.float8_e4m3fn, 7), "e5m2": (ml_dtypes.float8_e5m2, 14)}[fmt]
    v = np.moveaxis(np.asarray(x, np.float32).astype(ml_dtypes.bfloat16).astype(np.float64), axis, -1)
    blocks = v.reshape(v.shape[:-1] + (-1, 32))
    amax = np.abs(blocks).max(-1, keepdims=True)
    byte = np.maximum(np.where(amax > 0, np.frexp(amax)[1] - 1 + 127, 0) - down, 1)
    scale = np.exp2(byte - 127.0)
    codes = (blocks / scale).astype(np.float32).astype(dtype).astype(np.float64)
    return np.moveaxis((codes * scale).reshape(v.shape), -1, axis)


WIDE = False


def mx_kscale(k):
    if not WIDE:
        return np.ones(k)
    levels = np.array([24, -24, 12, -12, 0])
    if k % 512:
        return np.exp2(np.random.permutation(np.resize(levels, k // 32))).repeat(32)
    a = np.empty((k // 512, 16))
    for p in range(k // 512):
        a[p, :8] = np.random.permutation(np.resize(levels, 8))
        for g in range(8):
            far = levels[np.abs(levels - a[p, g]) >= 10]
            a[p, g + 8] = far[np.random.randint(len(far))]
    return np.exp2(a.ravel()).repeat(32)


def f64(x):
    return np.asarray(x).astype(np.float64)


def striped(idx):
    return np.tile(idx.reshape(-1, 16).T, (8, 1)).astype(np.uint16)


def unstriped(offs):
    return offs[:16].T.reshape(-1).astype(np.int64)


E2M1 = np.array([0.0, 0.5, 1.0, 1.5, 2.0, 3.0, 4.0, 6.0, -0.0, -0.5, -1.0, -1.5, -2.0, -3.0, -4.0, -6.0])


def pack_weight(w, fmt):
    k, n = w.shape
    w = f64(np.asarray(w, np.float32).astype(ml_dtypes.bfloat16)).reshape(k // 32, 32, n)
    amax = np.abs(w).max(1)
    if fmt == "e4m3":
        byte = np.frexp(amax)[1] - 1 + 127 - 7
    else:
        mant, ex = np.frexp(amax / 6.0)
        byte = np.where(mant > 0.5, ex, ex - 1) + 127
    byte = np.clip(np.where(amax > 0, byte, 1), 1, 254)
    scaled = (w * np.exp2(127.0 - byte)[:, None, :]).reshape(k, n).astype(np.float32)
    by_word = np.ascontiguousarray(scaled.reshape(k // 512, 128, 4, n).transpose(0, 1, 3, 2))
    if fmt == "e4m3":
        words = by_word.astype(ml_dtypes.float8_e4m3fn).view(np.uint8)
    else:
        c = by_word.astype(ml_dtypes.float4_e2m1fn).view(np.uint8) & 0xF
        words = (c[..., 0::2] | (c[..., 1::2] << 4)).reshape(k // 512, 128, 2 * n)
    return np.ascontiguousarray(words), np.ascontiguousarray(byte.astype(np.uint8).reshape(k // 512, 16, n))


def unpack_weight(words, scales, fmt):
    g, _, n = scales.shape
    words = np.ascontiguousarray(words).reshape(g, 128, n, -1)
    if fmt == "e4m3":
        vals = words.view(ml_dtypes.float8_e4m3fn).astype(np.float64)
    else:
        nib = np.empty((g, 128, n, 4), np.uint8)
        nib[..., 0::2] = words & 0xF
        nib[..., 1::2] = words >> 4
        vals = E2M1[nib]
    vals = vals * np.repeat(np.exp2(scales.astype(np.float64) - 127.0), 8, axis=1)[..., None]
    return vals.transpose(0, 1, 3, 2).reshape(g * 512, n)


K, R, M, T, N, J = 512, 512, 256, 2048, 256, 1024


def setup_inputs():
    n = np.random.standard_normal
    u = mx_kscale(R)[:, None]
    s = mx_kscale(K)[:, None]
    p_w4 = pack_weight(n((K, R)) / np.sqrt(K) / s / u.T, "e2m1")
    p_tab = pack_weight(n((R, T)) * u, "e4m3")
    return {
        "x": (n((K, M)) * s).astype(np.float32),
        "w4_words": p_w4[0],
        "w4_scales": p_w4[1],
        "tab_words": p_tab[0],
        "tab_scales": p_tab[1],
        "wv": (n((R, N)) / np.sqrt(R) / u).astype(np.float32),
        "offs": striped(np.random.permutation(T)[:J]),
    }


def reference(x, w4_words, w4_scales, tab_words, tab_scales, wv, offs):
    idx = unstriped(offs)
    x_ = mxq(f64(x), 0, "e4m3")
    w4_ = unpack_weight(w4_words, w4_scales, "e2m1")
    qa = w4_.T @ x_
    qa_ = mxq(qa, 0, "e4m3")
    tab_ = unpack_weight(tab_words, tab_scales, "e4m3")[:, idx]
    sc = qa_.T @ tab_
    wv_ = mxq(f64(wv), 0, "e4m3")
    vv = wv_.T @ tab_
    return np.exp(sc * 0.015625), vv

@@ -1,0 +1,169 @@
+from contextlib import ExitStack
+
+import concourse.mybir as mybir
+
+K, R, M, T, N, J = 512, 512, 256, 2048, 256, 1024
+FLOPS = 2 * K * R * M + 2 * R * M * J + 2 * R * N * J
+
+F32 = mybir.dt.float32
+BF16 = mybir.dt.bfloat16
+I32 = mybir.dt.int32
+U32 = mybir.dt.uint32
+U16 = mybir.dt.uint16
+U8 = mybir.dt.uint8
+FP8X4 = mybir.dt.float8_e4m3fn_x4
+FP4X4 = mybir.dt.float4_e2m1fn_x4
+EXP = mybir.ActivationFunctionType.Exp
+
+P = 128
+PACK = 4
+PIECE = 256
+PIECES = J // PIECE
+SCORE_SCALE = 0.015625
+
+
+def tile_list_mlat_exp_kernel(
+    tc, x, w4_words, w4_scales, tab_words, tab_scales, wv, offs, out_0, out_1
+):
+    nc = tc.nc
+    with ExitStack() as ctx:
+        keep = ctx.enter_context(tc.tile_pool(name="keep", bufs=1))
+        psum = ctx.enter_context(tc.psum_pool(name="psum", bufs=1))
+
+        offsets = keep.tile([P, J // 16], U16, name="offsets")
+        tab_s = keep.tile([P, T], U8, name="tab_s", tag="tab_s", align_bytes=64)
+        w4_s = keep.tile([P, R], U8, name="w4_s", tag="w4_s", align_bytes=64)
+        w4_w = keep.tile([P, 2 * R], U8, name="w4_w", align_bytes=64)
+        x_raw = keep.tile([P, PACK, M], F32, name="x_raw", tag="x_raw", align_bytes=64)
+        tab_w = keep.tile([P, T], U32, name="tab_w", align_bytes=64)
+        warm_in = keep.tile([P, 1], F32, name="warm_in")
+        warm_out = keep.tile([P, 1], F32, name="warm_out")
+
+        nc.vector.memset(tab_s[:].bitcast(I32), 0)
+        nc.vector.memset(warm_in[:], 0.0)
+        nc.vector.memset(w4_s[64:128, :].bitcast(I32), 0)
+        nc.gpsimd.memset(w4_s[0:64, :].bitcast(I32), 0)
+
+        def load_scale_rows(queue, plane, rows, q):
+            queue.dma_start(
+                out=plane[32 * q : 32 * q + 4, :].bitcast(I32),
+                in_=rows[0, 4 * q : 4 * q + 4, :].bitcast(I32),
+            )
+
+        nc.sync.dma_start(offsets[:], offs)
+        nc.sync.dma_start(out=w4_w[:].bitcast(I32), in_=w4_words[0].bitcast(I32))
+        nc.sync.dma_start(out=x_raw[:], in_=x.rearrange("(p j) m -> p j m", j=PACK))
+        nc.sync.dma_start(
+            out=tab_w[:].bitcast(I32), in_=tab_words[0].rearrange("p t i -> p (t i)").bitcast(I32)
+        )
+        for q in range(4):
+            load_scale_rows(nc.scalar, tab_s, tab_scales, q)
+        nc.scalar.activation(out=warm_out[:], in_=warm_in[:], func=EXP)
+        for q in range(4):
+            load_scale_rows(nc.gpsimd if q < 2 else nc.scalar, w4_s, w4_scales, q)
+
+        w4_wp = keep.tile([P, 2 * R], U8, name="w4_wp", align_bytes=64)
+        w4_sp = keep.tile([P, R], U8, name="w4_sp", align_bytes=64)
+        nc.vector.tensor_copy(
+            out=w4_wp[:].bitcast(U16).rearrange("p (t q) -> p t q", t=PACK),
+            in_=w4_w[:].bitcast(U16).rearrange("p (q t) -> p t q", t=PACK),
+        )
+        nc.vector.tensor_copy(
+            out=w4_sp[:].rearrange("p (t q) -> p t q", t=PACK),
+            in_=w4_s[:].rearrange("p (q t) -> p t q", t=PACK),
+        )
+
+        def cast(engine_copy, raw, h, tag):
+            grouped = keep.tile([P, P * PACK], BF16, name=tag, tag=tag, align_bytes=64)
+            engine_copy(
+                out=grouped[:].rearrange("p (c i t) -> p c t i", i=4, t=PACK),
+                in_=raw[:, :, h * P : (h + 1) * P].rearrange("p t (c i) -> p c t i", i=4),
+            )
+            return grouped
+
+        def quantise(grouped, name, tag=None):
+            codes = keep.tile([P, P], U32, name=name + "_c", tag=tag or name + "_c", align_bytes=64)
+            scales = keep.tile([P, P], U8, name=name + "_s", align_bytes=64)
+            nc.vector.quantize_mx(out=codes[:].bitcast(FP8X4), scales=scales[:], in_=grouped[:])
+            return codes, scales
+
+        def gather(window, dtype, i, tag):
+            part = offsets[:, i * (PIECE // 16) : (i + 1) * (PIECE // 16)]
+            got = keep.tile([P, PIECE], dtype, name="got_" + tag, tag=tag, align_bytes=64)
+            nc.vector.tensor_copy(got[:], window[:].indirect(part))
+            return got
+
+        all_s = keep.tile([P, J], U8, name="all_s", align_bytes=64)
+        nc.vector.tensor_copy(all_s[:], tab_s[:].indirect(offsets[:]))
+        got_s = [all_s[:, i * PIECE : (i + 1) * PIECE] for i in range(PIECES)]
+        xq = [
+            quantise(cast(nc.scalar.copy, x_raw, h, "x_g%d" % h), "xq%d" % h, "tab_s" if h == 0 else None)
+            for h in range(2)
+        ]
+
+        wv_raw = keep.tile([P, PACK, N], F32, name="wv_raw", tag="x_raw", align_bytes=64)
+        nc.sync.dma_start(out=wv_raw[:], in_=wv.rearrange("(p j) n -> p j n", j=PACK))
+
+        qa = []
+        for h in range(2):
+            x_c, x_s = xq[h]
+            bank = psum.tile([P, PACK, P], F32, name="bank%d" % (6 + h))
+            for t in range(PACK):
+                nc.tensor.matmul_mx(
+                    out=bank[:, t, :],
+                    lhsT=w4_wp[:, 2 * P * t : 2 * P * (t + 1)].bitcast(FP4X4),
+                    lhsT_scale=w4_sp[:, P * t : P * (t + 1)],
+                    rhs=x_c[:].bitcast(FP8X4),
+                    rhs_scale=x_s[:],
+                    start=True,
+                    stop=True,
+                )
+            qa_g = keep.tile([P, P * PACK], BF16, name="qa_g%d" % h, tag="qa_g%d" % h, align_bytes=64)
+            nc.scalar.copy(
+                out=qa_g[:].rearrange("p (m t) -> p m t", t=PACK),
+                in_=bank[:].rearrange("p t m -> p m t"),
+            )
+            qa.append(quantise(qa_g, "qa%d" % h))
+
+        got_w = [gather(tab_w, U32, i, tag) for i, tag in enumerate(["w4_s", "qa_g0", "qa_g1"])]
+        wq = [quantise(cast(nc.vector.tensor_copy, wv_raw, h, "wv_g%d" % h), "wq%d" % h) for h in range(2)]
+        got_w.append(gather(tab_w, U32, 3, "wv_g1"))
+
+        def product(i, left, out):
+            nc.tensor.matmul_mx(
+                out=out,
+                lhsT=left[0][:].bitcast(FP8X4),
+                lhsT_scale=left[1][:],
+                rhs=got_w[i][:].bitcast(FP8X4),
+                rhs_scale=got_s[i],
+                start=True,
+                stop=True,
+            )
+
+        for h in range(2):
+            bank = psum.tile([P, PIECE], F32, name="bank%d" % h)
+            product(0, qa[h], bank[:])
+            res = keep.tile([P, PIECE], F32, name="res0_0%d" % h)
+            nc.scalar.activation(out=res[:], in_=bank[:], func=EXP, scale=SCORE_SCALE)
+            nc.sync.dma_start(out=out_0[h * P : (h + 1) * P, 0:PIECE], in_=res[:])
+        for i in range(1, PIECES):
+            bank = psum.tile([P, 2, PIECE], F32, name="bank%d" % (i + 1))
+            for h in range(2):
+                product(i, qa[h], bank[:, h, :])
+            res = keep.tile([P, 2, PIECE], F32, name="res0_%d" % i)
+            nc.scalar.activation(out=res[:], in_=bank[:], func=EXP, scale=SCORE_SCALE)
+            nc.sync.dma_start(
+                out=out_0[:, i * PIECE : (i + 1) * PIECE].rearrange("(h p) j -> p h j", h=2), in_=res[:]
+            )
+        for i in range(PIECES):
+            bank = psum.tile([P, 2, PIECE], F32, name="bank%d" % ((5 + i) % 8))
+            for h in range(2):
+                product(i, wq[h], bank[:, h, :])
+            res = keep.tile([P, 2, PIECE], F32, name="res1_%d" % i)
+            if i % 2 == 1:
+                nc.vector.tensor_copy(out=res[:], in_=bank[:])
+            else:
+                nc.scalar.copy(out=res[:], in_=bank[:])
+            nc.sync.dma_start(
+                out=out_1[:, i * PIECE : (i + 1) * PIECE].rearrange("(h p) j -> p h j", h=2), in_=res[:]
+            )

@@ -30,37 +30,44 @@ def tile_list_mlat_exp_kernel(
         keep = ctx.enter_context(tc.tile_pool(name="keep", bufs=1))
         psum = ctx.enter_context(tc.psum_pool(name="psum", bufs=1))
 
+        raw = ctx.enter_context(tc.tile_pool(name="raw", bufs=1))
+        mid = ctx.enter_context(tc.tile_pool(name="mid", bufs=1))
+        late = ctx.enter_context(tc.tile_pool(name="late", bufs=1))
+
         offsets = keep.tile([P, J // 16], U16, name="offsets")
-        tab_s = keep.tile([P, T], U8, name="tab_s", tag="tab_s", align_bytes=64)
-        w4_s = keep.tile([P, R], U8, name="w4_s", tag="w4_s", align_bytes=64)
+        tab_s = keep.tile([P, T], U8, name="tab_s", align_bytes=64)
+        w4_s = mid.tile([P, R], U8, name="w4_s", align_bytes=64, offset=960)
         w4_w = keep.tile([P, 2 * R], U8, name="w4_w", align_bytes=64)
-        x_raw = keep.tile([P, PACK, M], F32, name="x_raw", tag="x_raw", align_bytes=64)
-        tab_w = keep.tile([P, T], U32, name="tab_w", align_bytes=64)
-        warm_in = keep.tile([P, 1], F32, name="warm_in")
+        zeros = raw.tile([P, R // 4], I32, name="zeros", offset=4096 - 256)
+        warm_in = keep.tile([P, 1], F32, name="warm_in", tag="tab_w", align_bytes=64)
         warm_out = keep.tile([P, 1], F32, name="warm_out")
 
         nc.vector.memset(tab_s[:].bitcast(I32), 0)
+        nc.gpsimd.memset(zeros[:], 0)
+        nc.vector.tensor_copy(out=w4_s[:].bitcast(I32), in_=zeros[:])
         nc.vector.memset(warm_in[:], 0.0)
-        nc.vector.memset(w4_s[64:128, :].bitcast(I32), 0)
-        nc.gpsimd.memset(w4_s[0:64, :].bitcast(I32), 0)
+        nc.scalar.activation(out=warm_out[:], in_=warm_in[:], func=EXP)
 
-        def load_scale_rows(queue, plane, rows, q):
-            queue.dma_start(
-                out=plane[32 * q : 32 * q + 4, :].bitcast(I32),
-                in_=rows[0, 4 * q : 4 * q + 4, :].bitcast(I32),
-            )
+        x_raw = raw.tile([P, PACK, M], F32, name="x_raw", offset=0)
+        wv_raw = raw.tile([P, PACK, N], F32, name="wv_raw", offset=4096)
+        tab_w = keep.tile([P, T], U32, name="tab_w", tag="tab_w", align_bytes=64)
+
+        def load_scale_rows(plane, rows, on_scalar):
+            for q in range(4):
+                (nc.scalar if q in on_scalar else nc.sync).dma_start(
+                    out=plane[32 * q : 32 * q + 4, :].bitcast(I32),
+                    in_=rows[0, 4 * q : 4 * q + 4, :].bitcast(I32),
+                )
 
         nc.sync.dma_start(offsets[:], offs)
         nc.sync.dma_start(out=w4_w[:].bitcast(I32), in_=w4_words[0].bitcast(I32))
+        load_scale_rows(tab_s, tab_scales, (1,))
         nc.sync.dma_start(out=x_raw[:], in_=x.rearrange("(p j) m -> p j m", j=PACK))
+        nc.sync.dma_start(out=wv_raw[:], in_=wv.rearrange("(p j) n -> p j n", j=PACK))
+        load_scale_rows(w4_s, w4_scales, (1, 3))
         nc.sync.dma_start(
             out=tab_w[:].bitcast(I32), in_=tab_words[0].rearrange("p t i -> p (t i)").bitcast(I32)
         )
-        for q in range(4):
-            load_scale_rows(nc.scalar, tab_s, tab_scales, q)
-        nc.scalar.activation(out=warm_out[:], in_=warm_in[:], func=EXP)
-        for q in range(4):
-            load_scale_rows(nc.gpsimd if q < 2 else nc.scalar, w4_s, w4_scales, q)
 
         w4_wp = keep.tile([P, 2 * R], U8, name="w4_wp", align_bytes=64)
         w4_sp = keep.tile([P, R], U8, name="w4_sp", align_bytes=64)
@@ -73,36 +80,28 @@ def tile_list_mlat_exp_kernel(
             in_=w4_s[:].rearrange("p (q t) -> p t q", t=PACK),
         )
 
-        def cast(engine_copy, raw, h, tag):
+        def cast(engine_copy, rows, h, tag):
             grouped = keep.tile([P, P * PACK], BF16, name=tag, tag=tag, align_bytes=64)
             engine_copy(
                 out=grouped[:].rearrange("p (c i t) -> p c t i", i=4, t=PACK),
-                in_=raw[:, :, h * P : (h + 1) * P].rearrange("p t (c i) -> p c t i", i=4),
+                in_=rows[:, :, h * P : (h + 1) * P].rearrange("p t (c i) -> p c t i", i=4),
             )
             return grouped
 
-        def quantise(grouped, name, tag=None):
-            codes = keep.tile([P, P], U32, name=name + "_c", tag=tag or name + "_c", align_bytes=64)
-            scales = keep.tile([P, P], U8, name=name + "_s", align_bytes=64)
+        def quantise(grouped, name):
+            codes = keep.tile([P, P], U32, name=name + "_c", align_bytes=64)
+            if name in ("xq1", "wq0"):
+                at = 1280 if name == "xq1" else 1408
+                scales = mid.tile([P, P], U8, name=name + "_s", align_bytes=64, offset=at)
+            else:
+                scales = keep.tile([P, P], U8, name=name + "_s", align_bytes=64)
             nc.vector.quantize_mx(out=codes[:].bitcast(FP8X4), scales=scales[:], in_=grouped[:])
             return codes, scales
 
-        def gather(window, dtype, i, tag):
-            part = offsets[:, i * (PIECE // 16) : (i + 1) * (PIECE // 16)]
-            got = keep.tile([P, PIECE], dtype, name="got_" + tag, tag=tag, align_bytes=64)
-            nc.vector.tensor_copy(got[:], window[:].indirect(part))
-            return got
+        def gather(got, window, first, last):
+            nc.vector.tensor_copy(got[:], window[:].indirect(offsets[:, first // 16 : last // 16]))
 
-        all_s = keep.tile([P, J], U8, name="all_s", align_bytes=64)
-        nc.vector.tensor_copy(all_s[:], tab_s[:].indirect(offsets[:]))
-        got_s = [all_s[:, i * PIECE : (i + 1) * PIECE] for i in range(PIECES)]
-        xq = [
-            quantise(cast(nc.scalar.copy, x_raw, h, "x_g%d" % h), "xq%d" % h, "tab_s" if h == 0 else None)
-            for h in range(2)
-        ]
-
-        wv_raw = keep.tile([P, PACK, N], F32, name="wv_raw", tag="x_raw", align_bytes=64)
-        nc.sync.dma_start(out=wv_raw[:], in_=wv.rearrange("(p j) n -> p j n", j=PACK))
+        xq = [quantise(cast(nc.scalar.copy, x_raw, h, "x_g%d" % h), "xq%d" % h) for h in range(2)]
 
         qa = []
         for h in range(2):
@@ -118,52 +117,69 @@ def tile_list_mlat_exp_kernel(
                     start=True,
                     stop=True,
                 )
-            qa_g = keep.tile([P, P * PACK], BF16, name="qa_g%d" % h, tag="qa_g%d" % h, align_bytes=64)
+            qa_g = late.tile([P, P * PACK], BF16, name="qa_g%d" % h, align_bytes=64, offset=1536 * h)
             nc.scalar.copy(
                 out=qa_g[:].rearrange("p (m t) -> p m t", t=PACK),
                 in_=bank[:].rearrange("p t m -> p m t"),
             )
             qa.append(quantise(qa_g, "qa%d" % h))
 
-        got_w = [gather(tab_w, U32, i, tag) for i, tag in enumerate(["w4_s", "qa_g0", "qa_g1"])]
-        wq = [quantise(cast(nc.vector.tensor_copy, wv_raw, h, "wv_g%d" % h), "wq%d" % h) for h in range(2)]
-        got_w.append(gather(tab_w, U32, 3, "wv_g1"))
+        wv_g = keep.tile([P, P * PACK], BF16, name="wv_g", align_bytes=64)
+        wv_g2 = mid.tile([P, P * PACK], BF16, name="wv_g2", align_bytes=64, offset=0)
+        wq = []
+        for h, (engine_copy, grouped) in enumerate([(nc.scalar.copy, wv_g), (nc.vector.tensor_copy, wv_g2)]):
+            engine_copy(
+                out=grouped[:].rearrange("p (c i t) -> p c t i", i=4, t=PACK),
+                in_=wv_raw[:, :, h * P : (h + 1) * P].rearrange("p t (c i) -> p c t i", i=4),
+            )
+            c, s = quantise(grouped, "wq%d" % h)
+            wq.append((c[:], s[:]))
+        qa = [(c[:], s[:]) for c, s in qa]
+
+        early_s = keep.tile([P, 3 * PIECE], U8, name="early_s", align_bytes=64)
+        last_s = mid.tile([P, PIECE], U8, name="last_s", align_bytes=64, offset=1024)
+        gather(early_s, tab_s, 0, 3 * PIECE)
+        gather(last_s, tab_s, 3 * PIECE, J)
+        got_s = [early_s[:, i * PIECE : (i + 1) * PIECE] for i in range(3)] + [last_s[:]]
+        got_w = []
+        for i in range(PIECES):
+            got = late.tile(
+                [P, PIECE], U32, name="got_w%d" % i, align_bytes=64, offset=1024 * ((i - 1) % PIECES)
+            )
+            gather(got, tab_w, i * PIECE, (i + 1) * PIECE)
+            got_w.append(got)
 
         def product(i, left, out):
             nc.tensor.matmul_mx(
                 out=out,
-                lhsT=left[0][:].bitcast(FP8X4),
-                lhsT_scale=left[1][:],
+                lhsT=left[0].bitcast(FP8X4),
+                lhsT_scale=left[1],
                 rhs=got_w[i][:].bitcast(FP8X4),
                 rhs_scale=got_s[i],
                 start=True,
                 stop=True,
             )
 
+        def exp_out(out, in_):
+            nc.scalar.activation(out=out, in_=in_, func=EXP, scale=SCORE_SCALE)
+
         for h in range(2):
-            bank = psum.tile([P, PIECE], F32, name="bank%d" % h)
-            product(0, qa[h], bank[:])
-            res = keep.tile([P, PIECE], F32, name="res0_0%d" % h)
-            nc.scalar.activation(out=res[:], in_=bank[:], func=EXP, scale=SCORE_SCALE)
-            nc.sync.dma_start(out=out_0[h * P : (h + 1) * P, 0:PIECE], in_=res[:])
-        for i in range(1, PIECES):
-            bank = psum.tile([P, 2, PIECE], F32, name="bank%d" % (i + 1))
+            bank = psum.tile([P, PIECE], F32, name="bank%d" % (6 * h))
+            product(0, wq[h], bank[:])
+            res = keep.tile([P, PIECE], F32, name="res_first%d" % h)
+            nc.scalar.copy(out=res[:], in_=bank[:])
+            nc.sync.dma_start(out=out_1[h * P : (h + 1) * P, 0:PIECE], in_=res[:])
+        banks = [1, 2, 3, 4, 5, 7, 0]
+        jobs = [(0, 1), (1, 0), (1, 1), (2, 0), (2, 1), (3, 0), (3, 1)]
+        for b, (i, which) in zip(banks, jobs):
+            cols = slice(i * PIECE, (i + 1) * PIECE)
+            left, dest = [(wq, out_1), (qa, out_0)][which]
+            bank = psum.tile([P, 2, PIECE], F32, name="bank%d" % b)
             for h in range(2):
-                product(i, qa[h], bank[:, h, :])
-            res = keep.tile([P, 2, PIECE], F32, name="res0_%d" % i)
-            nc.scalar.activation(out=res[:], in_=bank[:], func=EXP, scale=SCORE_SCALE)
-            nc.sync.dma_start(
-                out=out_0[:, i * PIECE : (i + 1) * PIECE].rearrange("(h p) j -> p h j", h=2), in_=res[:]
-            )
-        for i in range(PIECES):
-            bank = psum.tile([P, 2, PIECE], F32, name="bank%d" % ((5 + i) % 8))
-            for h in range(2):
-                product(i, wq[h], bank[:, h, :])
-            res = keep.tile([P, 2, PIECE], F32, name="res1_%d" % i)
-            if i % 2 == 1:
-                nc.vector.tensor_copy(out=res[:], in_=bank[:])
+                product(i, left[h], bank[:, h, :])
+            res = keep.tile([P, 2, PIECE], F32, name="res%d_%d" % (which, i))
+            if which == 1:
+                exp_out(res[:], bank[:])
             else:
-                nc.scalar.copy(out=res[:], in_=bank[:])
-            nc.sync.dma_start(
-                out=out_1[:, i * PIECE : (i + 1) * PIECE].rearrange("(h p) j -> p h j", h=2), in_=res[:]
-            )
+                nc.vector.tensor_copy(out=res[:], in_=bank[:])
+            nc.sync.dma_start(out=dest[:, cols].rearrange("(h p) j -> p h j", h=2), in_=res[:])

@@ -38,19 +38,17 @@ def tile_list_mlat_exp_kernel(
         tab_s = keep.tile([P, T], U8, name="tab_s", align_bytes=64)
         w4_s = mid.tile([P, R], U8, name="w4_s", align_bytes=64, offset=960)
         w4_w = keep.tile([P, 2 * R], U8, name="w4_w", align_bytes=64)
-        zeros = raw.tile([P, R // 4], I32, name="zeros", offset=4096 - 256)
-        warm_in = keep.tile([P, 1], F32, name="warm_in", tag="tab_w", align_bytes=64)
-        warm_out = keep.tile([P, 1], F32, name="warm_out")
+        zeros = raw.tile([P, 2, 1024], I32, name="zeros", align_bytes=64, offset=4096 - 128)
 
         nc.vector.memset(tab_s[:].bitcast(I32), 0)
-        nc.gpsimd.memset(zeros[:], 0)
-        nc.vector.tensor_copy(out=w4_s[:].bitcast(I32), in_=zeros[:])
-        nc.vector.memset(warm_in[:], 0.0)
-        nc.scalar.activation(out=warm_out[:], in_=warm_in[:], func=EXP)
+        nc.gpsimd.memset(zeros[:, :, 0:64], 0)
+        nc.vector.tensor_copy(
+            out=w4_s[:].bitcast(I32).rearrange("p (a b) -> p a b", a=2), in_=zeros[:, :, 0:64]
+        )
 
         x_raw = raw.tile([P, PACK, M], F32, name="x_raw", offset=0)
         wv_raw = raw.tile([P, PACK, N], F32, name="wv_raw", offset=4096)
-        tab_w = keep.tile([P, T], U32, name="tab_w", tag="tab_w", align_bytes=64)
+        tab_w = raw.tile([P, T], U32, name="tab_w", align_bytes=64, offset=8192)
 
         def load_scale_rows(plane, rows, on_scalar):
             for q in range(4):
@@ -64,7 +62,7 @@ def tile_list_mlat_exp_kernel(
         load_scale_rows(tab_s, tab_scales, (1,))
         nc.sync.dma_start(out=x_raw[:], in_=x.rearrange("(p j) m -> p j m", j=PACK))
         nc.sync.dma_start(out=wv_raw[:], in_=wv.rearrange("(p j) n -> p j n", j=PACK))
-        load_scale_rows(w4_s, w4_scales, (1, 3))
+        load_scale_rows(w4_s, w4_scales, ())
         nc.sync.dma_start(
             out=tab_w[:].bitcast(I32), in_=tab_words[0].rearrange("p t i -> p (t i)").bitcast(I32)
         )

from contextlib import ExitStack

import concourse.mybir as mybir

K, R, M, T, N, J = 512, 512, 256, 2048, 256, 1024
FLOPS = 2 * K * R * M + 2 * R * M * J + 2 * R * N * J

F32 = mybir.dt.float32
BF16 = mybir.dt.bfloat16
I32 = mybir.dt.int32
U32 = mybir.dt.uint32
U16 = mybir.dt.uint16
U8 = mybir.dt.uint8
FP8X4 = mybir.dt.float8_e4m3fn_x4
FP4X4 = mybir.dt.float4_e2m1fn_x4
EXP = mybir.ActivationFunctionType.Exp

P = 128
PACK = 4
PIECE = 256
PIECES = J // PIECE
SCORE_SCALE = 0.015625


def tile_list_mlat_exp_kernel(
    tc, x, w4_words, w4_scales, tab_words, tab_scales, wv, offs, out_0, out_1
):
    nc = tc.nc
    with ExitStack() as ctx:
        keep = ctx.enter_context(tc.tile_pool(name="keep", bufs=1))
        psum = ctx.enter_context(tc.psum_pool(name="psum", bufs=1))

        raw = ctx.enter_context(tc.tile_pool(name="raw", bufs=1))
        mid = ctx.enter_context(tc.tile_pool(name="mid", bufs=1))
        late = ctx.enter_context(tc.tile_pool(name="late", bufs=1))

        offsets = keep.tile([P, J // 16], U16, name="offsets")
        tab_s = keep.tile([P, T], U8, name="tab_s", align_bytes=64)
        w4_s = mid.tile([P, R], U8, name="w4_s", align_bytes=64, offset=960)
        w4_w = keep.tile([P, 2 * R], U8, name="w4_w", align_bytes=64)
        zeros = raw.tile([P, 2, 1024], I32, name="zeros", align_bytes=64, offset=4096 - 128)

        nc.vector.memset(tab_s[:].bitcast(I32), 0)
        nc.gpsimd.memset(zeros[:, :, 0:64], 0)
        nc.vector.tensor_copy(
            out=w4_s[:].bitcast(I32).rearrange("p (a b) -> p a b", a=2), in_=zeros[:, :, 0:64]
        )

        x_raw = raw.tile([P, PACK, M], F32, name="x_raw", offset=0)
        wv_raw = raw.tile([P, PACK, N], F32, name="wv_raw", offset=4096)
        tab_w = raw.tile([P, T], U32, name="tab_w", align_bytes=64, offset=8192)

        def load_scale_rows(plane, rows, on_scalar):
            for q in range(4):
                (nc.scalar if q in on_scalar else nc.sync).dma_start(
                    out=plane[32 * q : 32 * q + 4, :].bitcast(I32),
                    in_=rows[0, 4 * q : 4 * q + 4, :].bitcast(I32),
                )

        nc.sync.dma_start(offsets[:], offs)
        nc.sync.dma_start(out=w4_w[:].bitcast(I32), in_=w4_words[0].bitcast(I32))
        load_scale_rows(tab_s, tab_scales, (1,))
        nc.sync.dma_start(out=x_raw[:], in_=x.rearrange("(p j) m -> p j m", j=PACK))
        nc.sync.dma_start(out=wv_raw[:], in_=wv.rearrange("(p j) n -> p j n", j=PACK))
        load_scale_rows(w4_s, w4_scales, ())
        nc.sync.dma_start(
            out=tab_w[:].bitcast(I32), in_=tab_words[0].rearrange("p t i -> p (t i)").bitcast(I32)
        )

        w4_wp = keep.tile([P, 2 * R], U8, name="w4_wp", align_bytes=64)
        w4_sp = keep.tile([P, R], U8, name="w4_sp", align_bytes=64)
        nc.vector.tensor_copy(
            out=w4_wp[:].bitcast(U16).rearrange("p (t q) -> p t q", t=PACK),
            in_=w4_w[:].bitcast(U16).rearrange("p (q t) -> p t q", t=PACK),
        )
        nc.vector.tensor_copy(
            out=w4_sp[:].rearrange("p (t q) -> p t q", t=PACK),
            in_=w4_s[:].rearrange("p (q t) -> p t q", t=PACK),
        )

        def cast(engine_copy, rows, h, tag):
            grouped = keep.tile([P, P * PACK], BF16, name=tag, tag=tag, align_bytes=64)
            engine_copy(
                out=grouped[:].rearrange("p (c i t) -> p c t i", i=4, t=PACK),
                in_=rows[:, :, h * P : (h + 1) * P].rearrange("p t (c i) -> p c t i", i=4),
            )
            return grouped

        def quantise(grouped, name):
            codes = keep.tile([P, P], U32, name=name + "_c", align_bytes=64)
            if name in ("xq1", "wq0"):
                at = 1280 if name == "xq1" else 1408
                scales = mid.tile([P, P], U8, name=name + "_s", align_bytes=64, offset=at)
            else:
                scales = keep.tile([P, P], U8, name=name + "_s", align_bytes=64)
            nc.vector.quantize_mx(out=codes[:].bitcast(FP8X4), scales=scales[:], in_=grouped[:])
            return codes, scales

        def gather(got, window, first, last):
            nc.vector.tensor_copy(got[:], window[:].indirect(offsets[:, first // 16 : last // 16]))

        xq = [quantise(cast(nc.scalar.copy, x_raw, h, "x_g%d" % h), "xq%d" % h) for h in range(2)]

        qa = []
        for h in range(2):
            x_c, x_s = xq[h]
            bank = psum.tile([P, PACK, P], F32, name="bank%d" % (6 + h))
            for t in range(PACK):
                nc.tensor.matmul_mx(
                    out=bank[:, t, :],
                    lhsT=w4_wp[:, 2 * P * t : 2 * P * (t + 1)].bitcast(FP4X4),
                    lhsT_scale=w4_sp[:, P * t : P * (t + 1)],
                    rhs=x_c[:].bitcast(FP8X4),
                    rhs_scale=x_s[:],
                    start=True,
                    stop=True,
                )
            qa_g = late.tile([P, P * PACK], BF16, name="qa_g%d" % h, align_bytes=64, offset=1536 * h)
            nc.scalar.copy(
                out=qa_g[:].rearrange("p (m t) -> p m t", t=PACK),
                in_=bank[:].rearrange("p t m -> p m t"),
            )
            qa.append(quantise(qa_g, "qa%d" % h))

        wv_g = keep.tile([P, P * PACK], BF16, name="wv_g", align_bytes=64)
        wv_g2 = mid.tile([P, P * PACK], BF16, name="wv_g2", align_bytes=64, offset=0)
        wq = []
        for h, (engine_copy, grouped) in enumerate([(nc.scalar.copy, wv_g), (nc.vector.tensor_copy, wv_g2)]):
            engine_copy(
                out=grouped[:].rearrange("p (c i t) -> p c t i", i=4, t=PACK),
                in_=wv_raw[:, :, h * P : (h + 1) * P].rearrange("p t (c i) -> p c t i", i=4),
            )
            c, s = quantise(grouped, "wq%d" % h)
            wq.append((c[:], s[:]))
        qa = [(c[:], s[:]) for c, s in qa]

        early_s = keep.tile([P, 3 * PIECE], U8, name="early_s", align_bytes=64)
        last_s = mid.tile([P, PIECE], U8, name="last_s", align_bytes=64, offset=1024)
        gather(early_s, tab_s, 0, 3 * PIECE)
        gather(last_s, tab_s, 3 * PIECE, J)
        got_s = [early_s[:, i * PIECE : (i + 1) * PIECE] for i in range(3)] + [last_s[:]]
        got_w = []
        for i in range(PIECES):
            got = late.tile(
                [P, PIECE], U32, name="got_w%d" % i, align_bytes=64, offset=1024 * ((i - 1) % PIECES)
            )
            gather(got, tab_w, i * PIECE, (i + 1) * PIECE)
            got_w.append(got)

        def product(i, left, out):
            nc.tensor.matmul_mx(
                out=out,
                lhsT=left[0].bitcast(FP8X4),
                lhsT_scale=left[1],
                rhs=got_w[i][:].bitcast(FP8X4),
                rhs_scale=got_s[i],
                start=True,
                stop=True,
            )

        def exp_out(out, in_):
            nc.scalar.activation(out=out, in_=in_, func=EXP, scale=SCORE_SCALE)

        for h in range(2):
            bank = psum.tile([P, PIECE], F32, name="bank%d" % (6 * h))
            product(0, wq[h], bank[:])
            res = keep.tile([P, PIECE], F32, name="res_first%d" % h)
            nc.scalar.copy(out=res[:], in_=bank[:])
            nc.sync.dma_start(out=out_1[h * P : (h + 1) * P, 0:PIECE], in_=res[:])
        banks = [1, 2, 3, 4, 5, 7, 0]
        jobs = [(0, 1), (1, 0), (1, 1), (2, 0), (2, 1), (3, 0), (3, 1)]
        for b, (i, which) in zip(banks, jobs):
            cols = slice(i * PIECE, (i + 1) * PIECE)
            left, dest = [(wq, out_1), (qa, out_0)][which]
            bank = psum.tile([P, 2, PIECE], F32, name="bank%d" % b)
            for h in range(2):
                product(i, left[h], bank[:, h, :])
            res = keep.tile([P, 2, PIECE], F32, name="res%d_%d" % (which, i))
            if which == 1:
                exp_out(res[:], bank[:])
            else:
                nc.vector.tensor_copy(out=res[:], in_=bank[:])
            nc.sync.dma_start(out=dest[:, cols].rearrange("(h p) j -> p h j", h=2), in_=res[:])
